import numpy as np
import ml_dtypes


def mxq(x, axis, fmt="e4m3"):
    dtype, down = {"e4m3": (ml_dtypes.float8_e4m3fn, 7), "e5m2": (ml_dtypes.float8_e5m2, 14)}[fmt]
    v = np.moveaxis(np.asarray(x, np.float32).astype(ml_dtypes.bfloat16).astype(np.float64), axis, -1)
    blocks = v.reshape(v.shape[:-1] + (-1, 32))
    amax = np.abs(blocks).max(-1, keepdims=True)
    byte = np.maximum(np.where(amax > 0, np.frexp(amax)[1] - 1 + 127, 0) - down, 1)
    scale = np.exp2(byte - 127.0)
    codes = (blocks / scale).astype(np.float32).astype(dtype).astype(np.float64)
    return np.moveaxis((codes * scale).reshape(v.shape), -1, axis)


WIDE = False


def mx_kscale(k):
    if not WIDE:
        return np.ones(k)
    levels = np.array([10, -10, 5, -5, 0])
    if k % 512:
        return np.exp2(np.random.permutation(np.resize(levels, k // 32))).repeat(32)
    a = np.empty((k // 512, 16))
    for p in range(k // 512):
        a[p, :8] = np.random.permutation(np.resize(levels, 8))
        for g in range(8):
            far = levels[np.abs(levels - a[p, g]) >= 10]
            a[p, g + 8] = far[np.random.randint(len(far))]
    return np.exp2(a.ravel()).repeat(32)


BF16 = ml_dtypes.bfloat16


def bf(x):
    return np.asarray(x, np.float32).astype(BF16)


def f64(x):
    return np.asarray(x).astype(np.float64)


B, C, G, P, D = 2, 1024, 1536, 1024, 512


def draw0():
    s, t = mx_kscale(G), mx_kscale(C)
    x = np.random.standard_normal((B, C, G)) * s * t[:, None]
    mix = np.random.standard_normal((G, P)) / np.sqrt(G) / s[:, None]
    static = 0.3 * np.random.standard_normal((C, P)) * t[:, None]
    w = np.random.standard_normal((D, C)) / np.sqrt(C) / t
    bias = 0.3 * np.random.standard_normal(D)
    return {"x": bf(x), "mix": bf(mix), "static": bf(static),
            "w": bf(w), "bias": bf(bias)}


def core(x, mix, static, w, bias):
    h = mxq(f64(x), 2, "e4m3") @ mxq(f64(mix), 0, "e4m3")
    z = np.maximum(h + f64(static), 0.0)
    y = mxq(f64(w), 1, "e4m3") @ mxq(z, 1, "e4m3")
    return y + f64(bias)[:, None]


def e4m3fn_bytes(y):
    return np.clip(np.asarray(y, np.float64), -448.0, 448.0).astype(np.float32).astype(ml_dtypes.float8_e4m3fn).view(np.uint8)


def e4m3fn_values(b):
    return np.asarray(b, np.uint8).view(ml_dtypes.float8_e4m3fn).astype(np.float64)


def setup_inputs():
    d = draw0()
    x0 = np.asarray(d['mix']).astype(np.float64)
    s = (np.max(np.abs(x0), axis=(1,), keepdims=True) / 448.0).astype(np.float32)
    out = {}
    for k, v in d.items():
        if k == 'mix':
            out['mix_bytes'] = e4m3fn_bytes(x0 / s.astype(np.float64))
            out['mix_scale'] = s
        else:
            out[k] = v
    return out


def reference(x, mix_bytes, mix_scale, static, w, bias):
    return core(x, e4m3fn_values(mix_bytes) * mix_scale.astype(np.float64), static, w, bias)

@@ -1,0 +1,265 @@
+from contextlib import ExitStack
+
+import concourse.mybir as mybir
+from concourse.masks import make_identity
+
+B, C, G, N, D = 2, 1024, 1536, 1024, 512
+FLOPS = 2 * B * C * G * N + 2 * B * D * C * N
+
+F32 = mybir.dt.float32
+BF16 = mybir.dt.bfloat16
+U32 = mybir.dt.uint32
+U8 = mybir.dt.uint8
+FP8 = mybir.dt.float8_e4m3fn
+FP8X4 = mybir.dt.float8_e4m3fn_x4
+ALU = mybir.AluOpType
+ACT = mybir.ActivationFunctionType
+ENG = mybir.EngineType
+
+P = 128
+PACK = 4
+KP = P * PACK
+X_PASSES = G // KP
+Z_PASSES = C // KP
+BLOCKS = ((0, 256), (256, 512), (768, 256))
+
+
+def tile_weather_grid_channel_mixing_s7_kernel(tc, x, mix_bytes, mix_scale, static, w, bias, out):
+    nc = tc.nc
+    with ExitStack() as ctx:
+        keep = ctx.enter_context(tc.tile_pool(name="keep", bufs=1))
+        stage = ctx.enter_context(tc.tile_pool(name="stage", bufs=3))
+        tps = ctx.enter_context(tc.psum_pool(name="tps", bufs=4))
+        accs = ctx.enter_context(tc.psum_pool(name="accs", bufs=4))
+
+        ident = keep.tile([P, P], F32, name="ident")
+        make_identity(nc, ident[:])
+
+        scale_sb = keep.tile([P, X_PASSES, PACK], F32, name="scale_sb")
+        mix_raw = [keep.tile([P, PACK, N], U8, name=f"mix_raw{c}", align_bytes=64) for c in range(X_PASSES)]
+        x_raw = [keep.tile([P, PACK, G], BF16, name=f"x_raw{q}", align_bytes=64) for q in range(4)]
+        static_sb = [keep.tile([P, PACK, N], BF16, name=f"static{g}", align_bytes=64) for g in range(Z_PASSES)]
+        w_raw = keep.tile([P, PACK, C], BF16, name="w_raw", align_bytes=64)
+        bias_bf = keep.tile([P, PACK], BF16, name="bias_bf")
+        bias_sb = keep.tile([P, PACK], F32, name="bias_sb")
+        warm = keep.tile([P, 1], F32, name="warm")
+
+        mix_codes = keep.tile([P, X_PASSES, N], U32, name="mix_codes", align_bytes=64)
+        mix_scales = keep.tile([P, X_PASSES, N], U8, name="mix_scales", align_bytes=64)
+        x_codes = keep.tile([P, 4, X_PASSES, KP], U32, name="x_codes", align_bytes=64)
+        x_scales = keep.tile([P, 4, X_PASSES, KP], U8, name="x_scales", align_bytes=64)
+        w_codes = keep.tile([P, Z_PASSES, D], U32, name="w_codes", align_bytes=64)
+        w_scales = keep.tile([P, Z_PASSES, D], U8, name="w_scales", align_bytes=64)
+
+        mix_v = mix_bytes.rearrange("(c p t) n -> c p t n", p=P, t=PACK)
+        x_v = x.rearrange("b (g m t) k -> b g m t k", m=P, t=PACK)
+        static_v = static.rearrange("(g p t) n -> g p t n", p=P, t=PACK)
+        out_v = out.rearrange("b (m j) n -> b m j n", j=PACK)
+
+        def load_x(q):
+            for pair in (0, 1):
+                ts = slice(2 * pair, 2 * pair + 2)
+                nc.sync.dma_start(out=x_raw[q][:, ts, :], in_=x_v[q // 2, q % 2][:, ts, :])
+
+        nc.sync.dma_start(out=scale_sb[:], in_=mix_scale.rearrange("(c p t) o -> p c (t o)", p=P, t=PACK))
+        nc.sync.dma_start(out=mix_raw[0][:], in_=mix_v[0])
+        load_x(0)
+        nc.sync.dma_start(out=mix_raw[1][:], in_=mix_v[1])
+        nc.sync.dma_start(out=mix_raw[2][:], in_=mix_v[2])
+        nc.sync.dma_start(out=static_sb[0][:], in_=static_v[0])
+        load_x(1)
+        nc.sync.dma_start(out=w_raw[:], in_=w.rearrange("(m j) c -> m j c", j=PACK))
+        nc.sync.dma_start(out=bias_bf[:], in_=bias.rearrange("(m j) -> m j", j=PACK))
+        nc.sync.dma_start(out=static_sb[1][:], in_=static_v[1])
+        load_x(2)
+        load_x(3)
+
+        nc.vector.memset(warm[:], 0.0)
+        nc.scalar.activation(out=warm[:], in_=warm[:], func=ACT.Relu)
+
+        def interleave(dst, src):
+            return (
+                dst.rearrange("p (c i) t -> p c t i", i=4),
+                src.rearrange("p t (c i) -> p c t i", i=4),
+            )
+
+        def mix_prep(blk, c):
+            n0, width = BLOCKS[blk]
+            cols = slice(n0, n0 + width)
+            planes = stage.tile([P, PACK, width], BF16, name="planes", align_bytes=64)
+            for t in range(PACK):
+                src = mix_raw[c][:, t, cols].bitcast(FP8)
+                scale = scale_sb[:, c, t : t + 1]
+                if blk == 0 and t % 2 == 0:
+                    nc.vector.tensor_scalar(out=planes[:, t, :], in0=src, scalar1=scale, scalar2=None, op0=ALU.mult)
+                else:
+                    nc.scalar.activation(out=planes[:, t, :], in_=src, func=ACT.Copy, scale=scale)
+            grouped = stage.tile([P, width, PACK], BF16, name="mix_grouped", align_bytes=64)
+            dst, src = interleave(grouped[:], planes[:])
+            nc.vector.tensor_copy(out=dst, in_=src)
+            nc.vector.quantize_mx(
+                out=mix_codes[:, c, cols].bitcast(FP8X4),
+                scales=mix_scales[:, c, cols],
+                in_=grouped[:].rearrange("p n t -> p (n t)"),
+            )
+
+        def turn(words, c, codes, scales, v_share):
+            grouped = stage.tile([P, PACK, P, PACK], BF16, name="turned", align_bytes=64)
+            gwords = grouped[:].rearrange("p j r t -> p (j r t)").bitcast(F32)
+            gwords = gwords.rearrange("p (h j r u) -> p h j r u", h=2, j=2, u=2)
+            for half in (0, 1):
+                bank = tps.tile([P, 2, 2, P], F32, name="bank")
+                for j in (0, 1):
+                    for u in (0, 1):
+                        nc.tensor.transpose(
+                            bank[:, j, u, :], words[:, 2 * half + j, 256 * c + u : 256 * (c + 1) : 2], ident[:]
+                        )
+                src = bank[:].rearrange("p j u r -> p j r u")
+                if half == 1 and v_share:
+                    nc.vector.tensor_copy(out=gwords[:, half], in_=src)
+                else:
+                    nc.scalar.copy(out=gwords[:, half], in_=src)
+            nc.vector.quantize_mx(
+                out=codes.bitcast(FP8X4), scales=scales, in_=grouped[:].rearrange("p j r t -> p (j r t)")
+            )
+
+        def turn_x(q, c):
+            turn(x_raw[q][:].bitcast(F32), c, x_codes[:, q, c, :], x_scales[:, q, c, :], q == 0)
+
+        def turn_w(g):
+            turn(w_raw[:].bitcast(F32), g, w_codes[:, g, :], w_scales[:, g, :], False)
+
+        z_planes = {}
+        z_quant = {}
+
+        def stage1(blk, q, pair):
+            n0, width = BLOCKS[blk]
+            cols = slice(n0, n0 + width)
+            if pair == 0:
+                z_planes[blk, q] = stage.tile([P, PACK, width], BF16, name="z_planes", align_bytes=64)
+            zp = z_planes[blk, q]
+            per_bank = 512 // width
+            for first in range(2 * pair, 2 * pair + 2, per_bank):
+                acc = accs.tile([P, per_bank, width], F32, name="acc")
+                for i in range(per_bank):
+                    m = slice((first + i) * P, (first + i + 1) * P)
+                    for c in range(X_PASSES):
+                        nc.tensor.matmul_mx(
+                            out=acc[:, i, :],
+                            lhsT=x_codes[:, q, c, m].bitcast(FP8X4),
+                            lhsT_scale=x_scales[:, q, c, m],
+                            rhs=mix_codes[:, c, cols].bitcast(FP8X4),
+                            rhs_scale=mix_scales[:, c, cols],
+                            start=(c == 0),
+                            stop=(c == X_PASSES - 1),
+                        )
+                ts = slice(first, first + per_bank)
+                nc.vector.tensor_tensor(out=zp[:, ts, :], in0=acc[:], in1=static_sb[q % 2][:, ts, cols], op=ALU.add)
+            if pair == 1:
+                grouped = stage.tile([P, width, PACK], BF16, name="z_grouped", align_bytes=64)
+                dst, src = interleave(grouped[:], zp[:])
+                if (blk == 1):
+                    nc.scalar.activation(out=dst, in_=src, func=ACT.Relu)
+                else:
+                    nc.vector.tensor_scalar(out=dst, in0=src, scalar1=0.0, scalar2=None, op0=ALU.max)
+                codes = stage.tile([P, width], U32, name="z_codes", bufs=6, align_bytes=64)
+                scales = stage.tile([P, width], U8, name="z_scales", bufs=6, align_bytes=64)
+                nc.vector.quantize_mx(
+                    out=codes[:].bitcast(FP8X4), scales=scales[:], in_=grouped[:].rearrange("p n t -> p (n t)")
+                )
+                z_quant[blk, q] = (codes, scales)
+
+        def stage2(blk, b, pair):
+            n0, width = BLOCKS[blk]
+            per_bank = 512 // width
+            osb = stage.tile([P, 2, width], F32, name="osb", bufs=4)
+            for first in range(0, 2, per_bank):
+                acc = accs.tile([P, per_bank, width], F32, name="acc")
+                for i in range(per_bank):
+                    j = 2 * pair + first + i
+                    m = slice(j * P, (j + 1) * P)
+                    for g in range(Z_PASSES):
+                        codes, scales = z_quant[blk, 2 * b + g]
+                        nc.tensor.matmul_mx(
+                            out=acc[:, i, :],
+                            lhsT=w_codes[:, g, m].bitcast(FP8X4),
+                            lhsT_scale=w_scales[:, g, m],
+                            rhs=codes[:].bitcast(FP8X4),
+                            rhs_scale=scales[:],
+                            start=(g == 0),
+                            stop=(g == Z_PASSES - 1),
+                        )
+                for i in range(per_bank):
+                    j = 2 * pair + first + i
+                    if not (blk == 2 and pair == 1 and b == 1):
+                        nc.scalar.activation(
+                            out=osb[:, first + i, :], in_=acc[:, i, :], func=ACT.Identity, bias=bias_sb[:, j : j + 1]
+                        )
+                    else:
+                        nc.vector.tensor_scalar(
+                            out=osb[:, first + i, :], in0=acc[:, i, :], scalar1=bias_sb[:, j : j + 1], scalar2=None, op0=ALU.add
+                        )
+            nc.sync.dma_start(out=out_v[b][:, 2 * pair : 2 * pair + 2, n0 : n0 + width], in_=osb[:])
+
+        with tc.manual_schedule(engines={ENG.PE}):
+            mix_prep(0, 0)
+            turn_x(0, 0)
+            turn_x(0, 1)
+            mix_prep(0, 1)
+            turn_x(0, 2)
+            mix_prep(0, 2)
+            nc.gpsimd.tensor_copy(out=bias_sb[:], in_=bias_bf[:])
+
+            turn_x(1, 0)
+            stage1(0, 0, 0)
+            turn_x(1, 1)
+            stage1(0, 0, 1)
+            turn_x(1, 2)
+            mix_prep(1, 0)
+            turn_w(0)
+            stage1(0, 1, 0)
+            turn_w(1)
+            stage1(0, 1, 1)
+            turn_x(2, 0)
+            turn_x(2, 1)
+            stage2(0, 0, 0)
+            mix_prep(1, 1)
+            turn_x(2, 2)
+            stage2(0, 0, 1)
+            turn_x(3, 0)
+            stage1(0, 2, 0)
+            turn_x(3, 1)
+            stage1(0, 2, 1)
+            turn_x(3, 2)
+            mix_prep(1, 2)
+            stage1(1, 0, 0)
+            stage1(1, 0, 1)
+            mix_prep(2, 0)
+            stage1(0, 3, 0)
+            stage1(0, 3, 1)
+            stage1(1, 1, 0)
+            stage1(1, 1, 1)
+            mix_prep(2, 1)
+            stage2(0, 1, 0)
+            stage2(0, 1, 1)
+            stage1(1, 2, 0)
+            stage1(1, 2, 1)
+            mix_prep(2, 2)
+            stage2(1, 0, 0)
+            stage2(1, 0, 1)
+            stage1(1, 3, 0)
+            stage1(1, 3, 1)
+            stage1(2, 0, 0)
+            stage1(2, 0, 1)
+            stage2(1, 1, 0)
+            stage2(1, 1, 1)
+            stage1(2, 1, 0)
+            stage1(2, 1, 1)
+            stage1(2, 2, 0)
+            stage1(2, 2, 1)
+            stage2(2, 0, 0)
+            stage2(2, 0, 1)
+            stage1(2, 3, 0)
+            stage1(2, 3, 1)
+            stage2(2, 1, 0)
+            stage2(2, 1, 1)

@@ -21,16 +21,15 @@ PACK = 4
 KP = P * PACK
 X_PASSES = G // KP
 Z_PASSES = C // KP
-BLOCKS = ((0, 256), (256, 512), (768, 256))
+BLOCKS = ((0, 256), (256, 256), (512, 256), (768, 256))
+V_COLS = {256:128}
 
 
 def tile_weather_grid_channel_mixing_s7_kernel(tc, x, mix_bytes, mix_scale, static, w, bias, out):
     nc = tc.nc
     with ExitStack() as ctx:
         keep = ctx.enter_context(tc.tile_pool(name="keep", bufs=1))
-        stage = ctx.enter_context(tc.tile_pool(name="stage", bufs=3))
-        tps = ctx.enter_context(tc.psum_pool(name="tps", bufs=4))
-        accs = ctx.enter_context(tc.psum_pool(name="accs", bufs=4))
+        psum = ctx.enter_context(tc.psum_pool(name="psum", bufs=1))
 
         ident = keep.tile([P, P], F32, name="ident")
         make_identity(nc, ident[:])
@@ -51,101 +50,117 @@ def tile_weather_grid_channel_mixing_s7_kernel(tc, x, mix_bytes, mix_scale, stat
         w_codes = keep.tile([P, Z_PASSES, D], U32, name="w_codes", align_bytes=64)
         w_scales = keep.tile([P, Z_PASSES, D], U8, name="w_scales", align_bytes=64)
 
+        wmax = max(width for n0, width in BLOCKS)
+        rings = {
+            "planes": [keep.tile([P, PACK * wmax], BF16, name=f"planes{i}", align_bytes=64) for i in range(3)],
+            "mixg": [keep.tile([P, PACK * wmax], BF16, name=f"mixg{i}", align_bytes=64) for i in range(3)],
+            "turned": [keep.tile([P, PACK * KP], BF16, name=f"turned{i}", align_bytes=64) for i in range(3)],
+            "zp": [keep.tile([P, PACK * wmax], BF16, name=f"zp{i}", align_bytes=64) for i in range(3)],
+            "zg": [keep.tile([P, PACK * wmax], BF16, name=f"zg{i}", align_bytes=64) for i in range(3)],
+            "zc": [keep.tile([P, wmax], U32, name=f"zc{i}", align_bytes=64) for i in range(6)],
+            "zs": [keep.tile([P, wmax], U8, name=f"zs{i}", align_bytes=64) for i in range(6)],
+            "osb": [keep.tile([P, 2 * wmax], F32, name=f"osb{i}", align_bytes=64) for i in range(4)],
+            "bank": [psum.tile([P, 512], F32, name=f"bank{i}") for i in range(8)],
+        }
+        used = {}
+        held = {}
+
+        def take(ring, key):
+            if (ring, key) not in held:
+                n = used.get(ring, 0)
+                used[ring] = n + 1
+                held[ring, key] = rings[ring][n % len(rings[ring])]
+            return held[ring, key]
+
         mix_v = mix_bytes.rearrange("(c p t) n -> c p t n", p=P, t=PACK)
         x_v = x.rearrange("b (g m t) k -> b g m t k", m=P, t=PACK)
         static_v = static.rearrange("(g p t) n -> g p t n", p=P, t=PACK)
         out_v = out.rearrange("b (m j) n -> b m j n", j=PACK)
 
-        def load_x(q):
-            for pair in (0, 1):
-                ts = slice(2 * pair, 2 * pair + 2)
-                nc.sync.dma_start(out=x_raw[q][:, ts, :], in_=x_v[q // 2, q % 2][:, ts, :])
+        def LX(q, pair):
+            ts = slice(2 * pair, 2 * pair + 2)
+            nc.sync.dma_start(out=x_raw[q][:, ts, :], in_=x_v[q // 2, q % 2][:, ts, :])
 
-        nc.sync.dma_start(out=scale_sb[:], in_=mix_scale.rearrange("(c p t) o -> p c (t o)", p=P, t=PACK))
-        nc.sync.dma_start(out=mix_raw[0][:], in_=mix_v[0])
-        load_x(0)
-        nc.sync.dma_start(out=mix_raw[1][:], in_=mix_v[1])
-        nc.sync.dma_start(out=mix_raw[2][:], in_=mix_v[2])
-        nc.sync.dma_start(out=static_sb[0][:], in_=static_v[0])
-        load_x(1)
-        nc.sync.dma_start(out=w_raw[:], in_=w.rearrange("(m j) c -> m j c", j=PACK))
-        nc.sync.dma_start(out=bias_bf[:], in_=bias.rearrange("(m j) -> m j", j=PACK))
-        nc.sync.dma_start(out=static_sb[1][:], in_=static_v[1])
-        load_x(2)
-        load_x(3)
+        def LM(c, lo=0, hi=N):
+            nc.sync.dma_start(out=mix_raw[c][:, :, lo:hi], in_=mix_v[c][:, :, lo:hi])
 
-        nc.vector.memset(warm[:], 0.0)
-        nc.scalar.activation(out=warm[:], in_=warm[:], func=ACT.Relu)
+        def LS(g, lo, hi):
+            nc.sync.dma_start(out=static_sb[g][:, :, lo:hi], in_=static_v[g][:, :, lo:hi])
 
-        def interleave(dst, src):
-            return (
-                dst.rearrange("p (c i) t -> p c t i", i=4),
-                src.rearrange("p t (c i) -> p c t i", i=4),
-            )
+        def LW():
+            nc.sync.dma_start(out=w_raw[:], in_=w.rearrange("(m j) c -> m j c", j=PACK))
+            nc.sync.dma_start(out=bias_bf[:], in_=bias.rearrange("(m j) -> m j", j=PACK))
 
-        def mix_prep(blk, c):
+        def cols_of(blk):
             n0, width = BLOCKS[blk]
-            cols = slice(n0, n0 + width)
-            planes = stage.tile([P, PACK, width], BF16, name="planes", align_bytes=64)
+            return slice(n0, n0 + width), width
+
+        def planar(tile, width):
+            return tile[:, : PACK * width].rearrange("p (t n) -> p t n", t=PACK)
+
+        def interleave(dst, src, width, lo, hi):
+            d = dst[:, PACK * lo : PACK * hi].rearrange("p (c i t) -> p c t i", i=4, t=PACK)
+            s = planar(src, width)[:, :, lo:hi].rearrange("p t (c i) -> p c t i", i=4)
+            return d, s
+
+        def W(blk, c, on_v=()):
+            cols, width = cols_of(blk)
+            planes = planar(take("planes", (blk, c)), width)
             for t in range(PACK):
                 src = mix_raw[c][:, t, cols].bitcast(FP8)
                 scale = scale_sb[:, c, t : t + 1]
-                if blk == 0 and t % 2 == 0:
+                if t in on_v:
                     nc.vector.tensor_scalar(out=planes[:, t, :], in0=src, scalar1=scale, scalar2=None, op0=ALU.mult)
                 else:
                     nc.scalar.activation(out=planes[:, t, :], in_=src, func=ACT.Copy, scale=scale)
-            grouped = stage.tile([P, width, PACK], BF16, name="mix_grouped", align_bytes=64)
-            dst, src = interleave(grouped[:], planes[:])
-            nc.vector.tensor_copy(out=dst, in_=src)
+
+        def I(blk, c, on_s=False):
+            cols, width = cols_of(blk)
+            dst, src = interleave(take("mixg", (blk, c)), take("planes", (blk, c)), width, 0, width)
+            if on_s:
+                nc.scalar.copy(out=dst, in_=src)
+            else:
+                nc.vector.tensor_copy(out=dst, in_=src)
+
+        def MQ(blk, c):
+            cols, width = cols_of(blk)
             nc.vector.quantize_mx(
                 out=mix_codes[:, c, cols].bitcast(FP8X4),
                 scales=mix_scales[:, c, cols],
-                in_=grouped[:].rearrange("p n t -> p (n t)"),
+                in_=take("mixg", (blk, c))[:, : PACK * width],
             )
 
-        def turn(words, c, codes, scales, v_share):
-            grouped = stage.tile([P, PACK, P, PACK], BF16, name="turned", align_bytes=64)
-            gwords = grouped[:].rearrange("p j r t -> p (j r t)").bitcast(F32)
-            gwords = gwords.rearrange("p (h j r u) -> p h j r u", h=2, j=2, u=2)
-            for half in (0, 1):
-                bank = tps.tile([P, 2, 2, P], F32, name="bank")
-                for j in (0, 1):
-                    for u in (0, 1):
-                        nc.tensor.transpose(
-                            bank[:, j, u, :], words[:, 2 * half + j, 256 * c + u : 256 * (c + 1) : 2], ident[:]
-                        )
-                src = bank[:].rearrange("p j u r -> p j r u")
-                if half == 1 and v_share:
-                    nc.vector.tensor_copy(out=gwords[:, half], in_=src)
-                else:
-                    nc.scalar.copy(out=gwords[:, half], in_=src)
-            nc.vector.quantize_mx(
-                out=codes.bitcast(FP8X4), scales=scales, in_=grouped[:].rearrange("p j r t -> p (j r t)")
-            )
+        def T(q, c, half):
+            words = (w_raw if q == 4 else x_raw[q])[:].bitcast(F32)
+            bank = take("bank", ("T", q, c, half))[:].rearrange("p (j u r) -> p j u r", j=2, u=2)
+            for j in (0, 1):
+                for u in (0, 1):
+                    nc.tensor.transpose(
+                        bank[:, j, u, :], words[:, 2 * half + j, 256 * c + u : 256 * (c + 1) : 2], ident[:]
+                    )
 
-        def turn_x(q, c):
-            turn(x_raw[q][:].bitcast(F32), c, x_codes[:, q, c, :], x_scales[:, q, c, :], q == 0)
+        def E(q, c, half, on_v=False):
+            gwords = take("turned", (q, c))[:].bitcast(F32).rearrange("p (h j r u) -> p h j r u", h=2, j=2, u=2)
+            src = take("bank", ("T", q, c, half))[:].rearrange("p (j u r) -> p j r u", j=2, u=2)
+            if on_v:
+                nc.vector.tensor_copy(out=gwords[:, half], in_=src)
+            else:
+                nc.scalar.copy(out=gwords[:, half], in_=src)
 
-        def turn_w(g):
-            turn(w_raw[:].bitcast(F32), g, w_codes[:, g, :], w_scales[:, g, :], False)
+        def Q(q, c):
+            codes, scales = (w_codes[:, c, :], w_scales[:, c, :]) if q == 4 else (x_codes[:, q, c, :], x_scales[:, q, c, :])
+            nc.vector.quantize_mx(out=codes.bitcast(FP8X4), scales=scales, in_=take("turned", (q, c))[:])
 
-        z_planes = {}
-        z_quant = {}
-
-        def stage1(blk, q, pair):
-            n0, width = BLOCKS[blk]
-            cols = slice(n0, n0 + width)
-            if pair == 0:
-                z_planes[blk, q] = stage.tile([P, PACK, width], BF16, name="z_planes", align_bytes=64)
-            zp = z_planes[blk, q]
+        def M(blk, q, pair):
+            cols, width = cols_of(blk)
             per_bank = 512 // width
             for first in range(2 * pair, 2 * pair + 2, per_bank):
-                acc = accs.tile([P, per_bank, width], F32, name="acc")
+                acc = take("bank", ("M", blk, q, first))
                 for i in range(per_bank):
                     m = slice((first + i) * P, (first + i + 1) * P)
                     for c in range(X_PASSES):
                         nc.tensor.matmul_mx(
-                            out=acc[:, i, :],
+                            out=acc[:, i * width : (i + 1) * width],
                             lhsT=x_codes[:, q, c, m].bitcast(FP8X4),
                             lhsT_scale=x_scales[:, q, c, m],
                             rhs=mix_codes[:, c, cols].bitcast(FP8X4),
@@ -153,113 +168,325 @@ def tile_weather_grid_channel_mixing_s7_kernel(tc, x, mix_bytes, mix_scale, stat
                             start=(c == 0),
                             stop=(c == X_PASSES - 1),
                         )
-                ts = slice(first, first + per_bank)
-                nc.vector.tensor_tensor(out=zp[:, ts, :], in0=acc[:], in1=static_sb[q % 2][:, ts, cols], op=ALU.add)
-            if pair == 1:
-                grouped = stage.tile([P, width, PACK], BF16, name="z_grouped", align_bytes=64)
-                dst, src = interleave(grouped[:], zp[:])
-                if (blk == 1):
-                    nc.scalar.activation(out=dst, in_=src, func=ACT.Relu)
-                else:
-                    nc.vector.tensor_scalar(out=dst, in0=src, scalar1=0.0, scalar2=None, op0=ALU.max)
-                codes = stage.tile([P, width], U32, name="z_codes", bufs=6, align_bytes=64)
-                scales = stage.tile([P, width], U8, name="z_scales", bufs=6, align_bytes=64)
-                nc.vector.quantize_mx(
-                    out=codes[:].bitcast(FP8X4), scales=scales[:], in_=grouped[:].rearrange("p n t -> p (n t)")
-                )
-                z_quant[blk, q] = (codes, scales)
 
-        def stage2(blk, b, pair):
-            n0, width = BLOCKS[blk]
+        def A(blk, q, pair):
+            cols, width = cols_of(blk)
             per_bank = 512 // width
-            osb = stage.tile([P, 2, width], F32, name="osb", bufs=4)
+            zp = planar(take("zp", (blk, q)), width)
+            for first in range(2 * pair, 2 * pair + 2, per_bank):
+                ts = slice(first, first + per_bank)
+                acc = take("bank", ("M", blk, q, first))[:].rearrange("p (t n) -> p t n", t=per_bank)
+                nc.vector.tensor_tensor(out=zp[:, ts, :], in0=acc, in1=static_sb[q % 2][:, ts, cols], op=ALU.add)
+
+        def R(blk, q):
+            cols, width = cols_of(blk)
+            v = V_COLS[width]
+            if v < width:
+                dst, src = interleave(take("zg", (blk, q)), take("zp", (blk, q)), width, v, width)
+                nc.scalar.activation(out=dst, in_=src, func=ACT.Relu)
+            if v > 0:
+                dst, src = interleave(take("zg", (blk, q)), take("zp", (blk, q)), width, 0, v)
+                nc.vector.tensor_scalar(out=dst, in0=src, scalar1=0.0, scalar2=None, op0=ALU.max)
+
+        def z_quant(blk, q):
+            cols, width = cols_of(blk)
+            return take("zc", (blk, q))[:, :width].bitcast(FP8X4), take("zs", (blk, q))[:, :width]
+
+        def ZQ(blk, q):
+            cols, width = cols_of(blk)
+            codes, scales = z_quant(blk, q)
+            nc.vector.quantize_mx(out=codes, scales=scales, in_=take("zg", (blk, q))[:, : PACK * width])
+
+        def S2(blk, b, pair):
+            cols, width = cols_of(blk)
+            per_bank = 1 if blk == len(BLOCKS) - 1 else 512 // width
             for first in range(0, 2, per_bank):
-                acc = accs.tile([P, per_bank, width], F32, name="acc")
-                for i in range(per_bank):
-                    j = 2 * pair + first + i
-                    m = slice(j * P, (j + 1) * P)
-                    for g in range(Z_PASSES):
-                        codes, scales = z_quant[blk, 2 * b + g]
-                        nc.tensor.matmul_mx(
-                            out=acc[:, i, :],
-                            lhsT=w_codes[:, g, m].bitcast(FP8X4),
-                            lhsT_scale=w_scales[:, g, m],
-                            rhs=codes[:].bitcast(FP8X4),
-                            rhs_scale=scales[:],
-                            start=(g == 0),
-                            stop=(g == Z_PASSES - 1),
-                        )
-                for i in range(per_bank):
-                    j = 2 * pair + first + i
-                    if not (blk == 2 and pair == 1 and b == 1):
-                        nc.scalar.activation(
-                            out=osb[:, first + i, :], in_=acc[:, i, :], func=ACT.Identity, bias=bias_sb[:, j : j + 1]
-                        )
-                    else:
-                        nc.vector.tensor_scalar(
-                            out=osb[:, first + i, :], in0=acc[:, i, :], scalar1=bias_sb[:, j : j + 1], scalar2=None, op0=ALU.add
-                        )
-            nc.sync.dma_start(out=out_v[b][:, 2 * pair : 2 * pair + 2, n0 : n0 + width], in_=osb[:])
+                take("bank", ("S", blk, b, pair, first))
+            order = [(i, g) for i in (0, 1) for g in range(Z_PASSES)]
+            if per_bank == 1:
+                order = [(i, g) for g in range(Z_PASSES) for i in (0, 1)]
+            for i, g in order:
+                acc = take("bank", ("S", blk, b, pair, i // per_bank * per_bank))
+                j = 2 * pair + i
+                m = slice(j * P, (j + 1) * P)
+                codes, scales = z_quant(blk, 2 * b + g)
+                nc.tensor.matmul_mx(
+                    out=acc[:, i % per_bank * width : (i % per_bank + 1) * width],
+                    lhsT=w_codes[:, g, m].bitcast(FP8X4),
+                    lhsT_scale=w_scales[:, g, m],
+                    rhs=codes,
+                    rhs_scale=scales,
+                    start=(g == 0),
+                    stop=(g == Z_PASSES - 1),
+                )
 
-        with tc.manual_schedule(engines={ENG.PE}):
-            mix_prep(0, 0)
-            turn_x(0, 0)
-            turn_x(0, 1)
-            mix_prep(0, 1)
-            turn_x(0, 2)
-            mix_prep(0, 2)
-            nc.gpsimd.tensor_copy(out=bias_sb[:], in_=bias_bf[:])
+        def O(blk, b, pair, on_v=()):
+            cols, width = cols_of(blk)
+            per_bank = 1 if blk == len(BLOCKS) - 1 else 512 // width
+            osb = take("osb", (blk, b, pair))[:, : 2 * width].rearrange("p (k n) -> p k n", k=2)
+            for k in (0, 1):
+                j = 2 * pair + k
+                acc = take("bank", ("S", blk, b, pair, k // per_bank * per_bank))
+                src = acc[:, k % per_bank * width : (k % per_bank + 1) * width]
+                if k in on_v:
+                    nc.vector.tensor_scalar(out=osb[:, k, :], in0=src, scalar1=bias_sb[:, j : j + 1], scalar2=None, op0=ALU.add)
+                else:
+                    nc.scalar.activation(out=osb[:, k, :], in_=src, func=ACT.Identity, bias=bias_sb[:, j : j + 1])
+            nc.sync.dma_start(out=out_v[b][:, 2 * pair : 2 * pair + 2, cols], in_=osb)
 
-            turn_x(1, 0)
-            stage1(0, 0, 0)
-            turn_x(1, 1)
-            stage1(0, 0, 1)
-            turn_x(1, 2)
-            mix_prep(1, 0)
-            turn_w(0)
-            stage1(0, 1, 0)
-            turn_w(1)
-            stage1(0, 1, 1)
-            turn_x(2, 0)
-            turn_x(2, 1)
-            stage2(0, 0, 0)
-            mix_prep(1, 1)
-            turn_x(2, 2)
-            stage2(0, 0, 1)
-            turn_x(3, 0)
-            stage1(0, 2, 0)
-            turn_x(3, 1)
-            stage1(0, 2, 1)
-            turn_x(3, 2)
-            mix_prep(1, 2)
-            stage1(1, 0, 0)
-            stage1(1, 0, 1)
-            mix_prep(2, 0)
-            stage1(0, 3, 0)
-            stage1(0, 3, 1)
-            stage1(1, 1, 0)
-            stage1(1, 1, 1)
-            mix_prep(2, 1)
-            stage2(0, 1, 0)
-            stage2(0, 1, 1)
-            stage1(1, 2, 0)
-            stage1(1, 2, 1)
-            mix_prep(2, 2)
-            stage2(1, 0, 0)
-            stage2(1, 0, 1)
-            stage1(1, 3, 0)
-            stage1(1, 3, 1)
-            stage1(2, 0, 0)
-            stage1(2, 0, 1)
-            stage2(1, 1, 0)
-            stage2(1, 1, 1)
-            stage1(2, 1, 0)
-            stage1(2, 1, 1)
-            stage1(2, 2, 0)
-            stage1(2, 2, 1)
-            stage2(2, 0, 0)
-            stage2(2, 0, 1)
-            stage1(2, 3, 0)
-            stage1(2, 3, 1)
-            stage2(2, 1, 0)
-            stage2(2, 1, 1)
+        nc.vector.memset(warm[:], 0.0)
+        nc.scalar.activation(out=warm[:], in_=warm[:], func=ACT.Relu)
+        nc.sync.dma_start(out=scale_sb[:], in_=mix_scale.rearrange("(c p t) o -> p c (t o)", p=P, t=PACK))
+        LM(0, 0, 512)
+        LX(0, 0)
+        LX(0, 1)
+        LM(1, 0, 512)
+        LM(2, 0, 512)
+        LX(1, 0)
+        LX(1, 1)
+        LW()
+        LX(2, 0)
+        LX(2, 1)
+        LS(0, 0, 1024)
+        LS(1, 0, 1024)
+        LX(3, 1)
+        LX(3, 0)
+        LM(1, 512, 1024)
+        LM(0, 512, 1024)
+        LM(2, 512, 1024)
+        nc.gpsimd.tensor_copy(out=bias_sb[:], in_=bias_bf[:])
+        with tc.manual_schedule():
+            W(0, 1, (0, 1, 2, 3,))
+            W(0, 0)
+            T(0, 0, 0)
+            T(0, 1, 0)
+            E(0, 0, 0)
+            T(0, 0, 1)
+            T(0, 2, 0)
+            E(0, 1, 0)
+            I(0, 0)
+            T(0, 2, 1)
+            W(0, 2, (0, 1, 2,))
+            T(0, 1, 1)
+            T(1, 0, 0)
+            E(0, 0, 1)
+            T(1, 2, 0)
+            E(0, 2, 0)
+            T(1, 1, 0)
+            MQ(0, 0)
+            Q(0, 0)
+            E(0, 1, 1)
+            E(1, 0, 0)
+            T(1, 2, 1)
+            I(0, 1)
+            T(1, 0, 1)
+            T(1, 1, 1)
+            W(1, 0, (0, 1, 2,))
+            Q(0, 1)
+            MQ(0, 1)
+            E(0, 2, 1, True)
+            T(4, 1, 1)
+            E(1, 2, 0)
+            I(0, 2)
+            E(1, 2, 1)
+            E(1, 0, 1)
+            T(4, 0, 1)
+            I(1, 0, True)
+            Q(0, 2)
+            E(1, 1, 0)
+            T(4, 0, 0)
+            T(4, 1, 0)
+            W(1, 2, (0, 1, 2, 3,))
+            MQ(0, 2)
+            M(0, 0, 1)
+            Q(1, 0)
+            I(1, 2, True)
+            MQ(1, 0)
+            E(4, 1, 1)
+            E(1, 1, 1, True)
+            Q(1, 1)
+            E(4, 1, 0)
+            W(1, 1, (0, 1, 2,))
+            Q(1, 2)
+            T(2, 2, 0)
+            E(4, 0, 0)
+            T(2, 0, 0)
+            A(0, 0, 1)
+            Q(4, 1)
+            E(4, 0, 1)
+            MQ(1, 2)
+            Q(4, 0)
+            E(2, 2, 0)
+            M(0, 0, 0)
+            M(0, 1, 1)
+            T(2, 2, 1)
+            E(2, 0, 0)
+            T(2, 0, 1)
+            M(0, 1, 0)
+            A(0, 0, 0)
+            A(0, 1, 1)
+            R(0, 0)
+            E(2, 2, 1, True)
+            T(2, 1, 0)
+            E(2, 0, 1)
+            A(0, 1, 0)
+            ZQ(0, 0)
+            Q(2, 0)
+            T(2, 1, 1)
+            I(1, 1, True)
+            T(3, 1, 1)
+            T(3, 2, 1)
+            MQ(1, 1)
+            T(3, 0, 0)
+            R(0, 1)
+            Q(2, 2)
+            ZQ(0, 1)
+            T(3, 2, 0)
+            E(2, 1, 1)
+            E(2, 1, 0)
+            T(3, 1, 0)
+            E(3, 2, 1)
+            S2(0, 0, 0)
+            T(3, 0, 1)
+            Q(2, 1)
+            W(2, 0, (0, 1, 2,))
+            S2(0, 0, 1)
+            E(3, 1, 1)
+            W(2, 2)
+            W(3, 0)
+            I(2, 2, True)
+            E(3, 2, 0, True)
+            E(3, 1, 0, True)
+            E(3, 0, 0, True)
+            E(3, 0, 1, True)
+            M(0, 2, 0)
+            O(0, 0, 0)
+            Q(3, 1)
+            M(0, 2, 1)
+            I(2, 0, True)
+            Q(3, 2)
+            Q(3, 0)
+            M(1, 1, 0)
+            M(0, 3, 0)
+            A(0, 2, 0)
+            M(0, 3, 1)
+            M(1, 0, 0)
+            A(0, 2, 1)
+            O(0, 0, 1)
+            M(1, 1, 1)
+            M(1, 2, 1)
+            A(0, 3, 0)
+            W(2, 1, (0,))
+            A(0, 3, 1)
+            M(1, 2, 0)
+            A(1, 1, 0)
+            R(0, 3)
+            R(0, 2)
+            MQ(2, 0)
+            MQ(2, 2)
+            ZQ(0, 3)
+            M(1, 0, 1)
+            M(1, 3, 1)
+            M(1, 3, 0)
+            W(3, 1, (0, 1,))
+            A(1, 2, 1)
+            A(1, 1, 1)
+            I(2, 1, True)
+            A(1, 0, 1)
+            I(3, 0, True)
+            MQ(2, 1)
+            A(1, 0, 0)
+            R(1, 1)
+            W(3, 2)
+            M(2, 0, 1)
+            A(1, 2, 0)
+            ZQ(1, 1)
+            ZQ(0, 2)
+            R(1, 0)
+            R(1, 2)
+            MQ(3, 0)
+            A(1, 3, 1)
+            M(2, 1, 0)
+            ZQ(1, 0)
+            M(2, 0, 0)
+            A(2, 0, 1)
+            I(3, 1, True)
+            I(3, 2, True)
+            S2(0, 1, 1)
+            M(2, 2, 1)
+            A(1, 3, 0)
+            MQ(3, 1)
+            M(2, 1, 1)
+            O(0, 1, 1)
+            S2(0, 1, 0)
+            A(2, 0, 0)
+            A(2, 1, 0)
+            MQ(3, 2)
+            ZQ(1, 2)
+            R(1, 3)
+            M(2, 2, 0)
+            M(2, 3, 0)
+            M(2, 3, 1)
+            M(3, 0, 0)
+            R(2, 0)
+            A(2, 2, 1)
+            S2(1, 0, 0)
+            M(3, 1, 1)
+            A(2, 2, 0)
+            A(2, 1, 1)
+            O(0, 1, 0)
+            M(3, 1, 0)
+            ZQ(1, 3)
+            R(2, 1)
+            A(2, 3, 1)
+            O(1, 0, 0)
+            S2(1, 0, 1)
+            ZQ(2, 1)
+            R(2, 2)
+            M(3, 0, 1)
+            A(2, 3, 0)
+            S2(1, 1, 1)
+            O(1, 0, 1)
+            S2(1, 1, 0)
+            A(3, 0, 0)
+            O(1, 1, 0)
+            A(3, 1, 1)
+            ZQ(2, 2)
+            ZQ(2, 0)
+            M(3, 3, 1)
+            R(2, 3)
+            M(3, 2, 0)
+            A(3, 0, 1)
+            A(3, 1, 0)
+            O(1, 1, 1)
+            ZQ(2, 3)
+            M(3, 3, 0)
+            A(3, 3, 1)
+            A(3, 3, 0)
+            S2(2, 1, 1)
+            R(3, 0)
+            R(3, 1)
+            S2(2, 0, 1)
+            ZQ(3, 0)
+            A(3, 2, 0)
+            O(2, 1, 1)
+            R(3, 3)
+            S2(2, 0, 0)
+            M(3, 2, 1)
+            O(2, 0, 0)
+            S2(2, 1, 0)
+            A(3, 2, 1)
+            ZQ(3, 1)
+            S2(3, 0, 0)
+            ZQ(3, 3)
+            O(2, 0, 1)
+            O(2, 1, 0)
+            R(3, 2)
+            S2(3, 0, 1)
+            O(3, 0, 0, (0,))
+            ZQ(3, 2)
+            S2(3, 1, 1)
+            O(3, 0, 1, (0,))
+            S2(3, 1, 0)
+            O(3, 1, 1, (0,))
+            O(3, 1, 0, (0,))

from contextlib import ExitStack

import concourse.mybir as mybir
from concourse.masks import make_identity

B, C, G, N, D = 2, 1024, 1536, 1024, 512
FLOPS = 2 * B * C * G * N + 2 * B * D * C * N

F32 = mybir.dt.float32
BF16 = mybir.dt.bfloat16
U32 = mybir.dt.uint32
U8 = mybir.dt.uint8
FP8 = mybir.dt.float8_e4m3fn
FP8X4 = mybir.dt.float8_e4m3fn_x4
ALU = mybir.AluOpType
ACT = mybir.ActivationFunctionType
ENG = mybir.EngineType

P = 128
PACK = 4
KP = P * PACK
X_PASSES = G // KP
Z_PASSES = C // KP
BLOCKS = ((0, 256), (256, 256), (512, 256), (768, 256))
V_COLS = {256:128}


def tile_weather_grid_channel_mixing_s7_kernel(tc, x, mix_bytes, mix_scale, static, w, bias, out):
    nc = tc.nc
    with ExitStack() as ctx:
        keep = ctx.enter_context(tc.tile_pool(name="keep", bufs=1))
        psum = ctx.enter_context(tc.psum_pool(name="psum", bufs=1))

        ident = keep.tile([P, P], F32, name="ident")
        make_identity(nc, ident[:])

        scale_sb = keep.tile([P, X_PASSES, PACK], F32, name="scale_sb")
        mix_raw = [keep.tile([P, PACK, N], U8, name=f"mix_raw{c}", align_bytes=64) for c in range(X_PASSES)]
        x_raw = [keep.tile([P, PACK, G], BF16, name=f"x_raw{q}", align_bytes=64) for q in range(4)]
        static_sb = [keep.tile([P, PACK, N], BF16, name=f"static{g}", align_bytes=64) for g in range(Z_PASSES)]
        w_raw = keep.tile([P, PACK, C], BF16, name="w_raw", align_bytes=64)
        bias_bf = keep.tile([P, PACK], BF16, name="bias_bf")
        bias_sb = keep.tile([P, PACK], F32, name="bias_sb")
        warm = keep.tile([P, 1], F32, name="warm")

        mix_codes = keep.tile([P, X_PASSES, N], U32, name="mix_codes", align_bytes=64)
        mix_scales = keep.tile([P, X_PASSES, N], U8, name="mix_scales", align_bytes=64)
        x_codes = keep.tile([P, 4, X_PASSES, KP], U32, name="x_codes", align_bytes=64)
        x_scales = keep.tile([P, 4, X_PASSES, KP], U8, name="x_scales", align_bytes=64)
        w_codes = keep.tile([P, Z_PASSES, D], U32, name="w_codes", align_bytes=64)
        w_scales = keep.tile([P, Z_PASSES, D], U8, name="w_scales", align_bytes=64)

        wmax = max(width for n0, width in BLOCKS)
        rings = {
            "planes": [keep.tile([P, PACK * wmax], BF16, name=f"planes{i}", align_bytes=64) for i in range(3)],
            "mixg": [keep.tile([P, PACK * wmax], BF16, name=f"mixg{i}", align_bytes=64) for i in range(3)],
            "turned": [keep.tile([P, PACK * KP], BF16, name=f"turned{i}", align_bytes=64) for i in range(3)],
            "zp": [keep.tile([P, PACK * wmax], BF16, name=f"zp{i}", align_bytes=64) for i in range(3)],
            "zg": [keep.tile([P, PACK * wmax], BF16, name=f"zg{i}", align_bytes=64) for i in range(3)],
            "zc": [keep.tile([P, wmax], U32, name=f"zc{i}", align_bytes=64) for i in range(6)],
            "zs": [keep.tile([P, wmax], U8, name=f"zs{i}", align_bytes=64) for i in range(6)],
            "osb": [keep.tile([P, 2 * wmax], F32, name=f"osb{i}", align_bytes=64) for i in range(4)],
            "bank": [psum.tile([P, 512], F32, name=f"bank{i}") for i in range(8)],
        }
        used = {}
        held = {}

        def take(ring, key):
            if (ring, key) not in held:
                n = used.get(ring, 0)
                used[ring] = n + 1
                held[ring, key] = rings[ring][n % len(rings[ring])]
            return held[ring, key]

        mix_v = mix_bytes.rearrange("(c p t) n -> c p t n", p=P, t=PACK)
        x_v = x.rearrange("b (g m t) k -> b g m t k", m=P, t=PACK)
        static_v = static.rearrange("(g p t) n -> g p t n", p=P, t=PACK)
        out_v = out.rearrange("b (m j) n -> b m j n", j=PACK)

        def LX(q, pair):
            ts = slice(2 * pair, 2 * pair + 2)
            nc.sync.dma_start(out=x_raw[q][:, ts, :], in_=x_v[q // 2, q % 2][:, ts, :])

        def LM(c, lo=0, hi=N):
            nc.sync.dma_start(out=mix_raw[c][:, :, lo:hi], in_=mix_v[c][:, :, lo:hi])

        def LS(g, lo, hi):
            nc.sync.dma_start(out=static_sb[g][:, :, lo:hi], in_=static_v[g][:, :, lo:hi])

        def LW():
            nc.sync.dma_start(out=w_raw[:], in_=w.rearrange("(m j) c -> m j c", j=PACK))
            nc.sync.dma_start(out=bias_bf[:], in_=bias.rearrange("(m j) -> m j", j=PACK))

        def cols_of(blk):
            n0, width = BLOCKS[blk]
            return slice(n0, n0 + width), width

        def planar(tile, width):
            return tile[:, : PACK * width].rearrange("p (t n) -> p t n", t=PACK)

        def interleave(dst, src, width, lo, hi):
            d = dst[:, PACK * lo : PACK * hi].rearrange("p (c i t) -> p c t i", i=4, t=PACK)
            s = planar(src, width)[:, :, lo:hi].rearrange("p t (c i) -> p c t i", i=4)
            return d, s

        def W(blk, c, on_v=()):
            cols, width = cols_of(blk)
            planes = planar(take("planes", (blk, c)), width)
            for t in range(PACK):
                src = mix_raw[c][:, t, cols].bitcast(FP8)
                scale = scale_sb[:, c, t : t + 1]
                if t in on_v:
                    nc.vector.tensor_scalar(out=planes[:, t, :], in0=src, scalar1=scale, scalar2=None, op0=ALU.mult)
                else:
                    nc.scalar.activation(out=planes[:, t, :], in_=src, func=ACT.Copy, scale=scale)

        def I(blk, c, on_s=False):
            cols, width = cols_of(blk)
            dst, src = interleave(take("mixg", (blk, c)), take("planes", (blk, c)), width, 0, width)
            if on_s:
                nc.scalar.copy(out=dst, in_=src)
            else:
                nc.vector.tensor_copy(out=dst, in_=src)

        def MQ(blk, c):
            cols, width = cols_of(blk)
            nc.vector.quantize_mx(
                out=mix_codes[:, c, cols].bitcast(FP8X4),
                scales=mix_scales[:, c, cols],
                in_=take("mixg", (blk, c))[:, : PACK * width],
            )

        def T(q, c, half):
            words = (w_raw if q == 4 else x_raw[q])[:].bitcast(F32)
            bank = take("bank", ("T", q, c, half))[:].rearrange("p (j u r) -> p j u r", j=2, u=2)
            for j in (0, 1):
                for u in (0, 1):
                    nc.tensor.transpose(
                        bank[:, j, u, :], words[:, 2 * half + j, 256 * c + u : 256 * (c + 1) : 2], ident[:]
                    )

        def E(q, c, half, on_v=False):
            gwords = take("turned", (q, c))[:].bitcast(F32).rearrange("p (h j r u) -> p h j r u", h=2, j=2, u=2)
            src = take("bank", ("T", q, c, half))[:].rearrange("p (j u r) -> p j r u", j=2, u=2)
            if on_v:
                nc.vector.tensor_copy(out=gwords[:, half], in_=src)
            else:
                nc.scalar.copy(out=gwords[:, half], in_=src)

        def Q(q, c):
            codes, scales = (w_codes[:, c, :], w_scales[:, c, :]) if q == 4 else (x_codes[:, q, c, :], x_scales[:, q, c, :])
            nc.vector.quantize_mx(out=codes.bitcast(FP8X4), scales=scales, in_=take("turned", (q, c))[:])

        def M(blk, q, pair):
            cols, width = cols_of(blk)
            per_bank = 512 // width
            for first in range(2 * pair, 2 * pair + 2, per_bank):
                acc = take("bank", ("M", blk, q, first))
                for i in range(per_bank):
                    m = slice((first + i) * P, (first + i + 1) * P)
                    for c in range(X_PASSES):
                        nc.tensor.matmul_mx(
                            out=acc[:, i * width : (i + 1) * width],
                            lhsT=x_codes[:, q, c, m].bitcast(FP8X4),
                            lhsT_scale=x_scales[:, q, c, m],
                            rhs=mix_codes[:, c, cols].bitcast(FP8X4),
                            rhs_scale=mix_scales[:, c, cols],
                            start=(c == 0),
                            stop=(c == X_PASSES - 1),
                        )

        def A(blk, q, pair):
            cols, width = cols_of(blk)
            per_bank = 512 // width
            zp = planar(take("zp", (blk, q)), width)
            for first in range(2 * pair, 2 * pair + 2, per_bank):
                ts = slice(first, first + per_bank)
                acc = take("bank", ("M", blk, q, first))[:].rearrange("p (t n) -> p t n", t=per_bank)
                nc.vector.tensor_tensor(out=zp[:, ts, :], in0=acc, in1=static_sb[q % 2][:, ts, cols], op=ALU.add)

        def R(blk, q):
            cols, width = cols_of(blk)
            v = V_COLS[width]
            if v < width:
                dst, src = interleave(take("zg", (blk, q)), take("zp", (blk, q)), width, v, width)
                nc.scalar.activation(out=dst, in_=src, func=ACT.Relu)
            if v > 0:
                dst, src = interleave(take("zg", (blk, q)), take("zp", (blk, q)), width, 0, v)
                nc.vector.tensor_scalar(out=dst, in0=src, scalar1=0.0, scalar2=None, op0=ALU.max)

        def z_quant(blk, q):
            cols, width = cols_of(blk)
            return take("zc", (blk, q))[:, :width].bitcast(FP8X4), take("zs", (blk, q))[:, :width]

        def ZQ(blk, q):
            cols, width = cols_of(blk)
            codes, scales = z_quant(blk, q)
            nc.vector.quantize_mx(out=codes, scales=scales, in_=take("zg", (blk, q))[:, : PACK * width])

        def S2(blk, b, pair):
            cols, width = cols_of(blk)
            per_bank = 1 if blk == len(BLOCKS) - 1 else 512 // width
            for first in range(0, 2, per_bank):
                take("bank", ("S", blk, b, pair, first))
            order = [(i, g) for i in (0, 1) for g in range(Z_PASSES)]
            if per_bank == 1:
                order = [(i, g) for g in range(Z_PASSES) for i in (0, 1)]
            for i, g in order:
                acc = take("bank", ("S", blk, b, pair, i // per_bank * per_bank))
                j = 2 * pair + i
                m = slice(j * P, (j + 1) * P)
                codes, scales = z_quant(blk, 2 * b + g)
                nc.tensor.matmul_mx(
                    out=acc[:, i % per_bank * width : (i % per_bank + 1) * width],
                    lhsT=w_codes[:, g, m].bitcast(FP8X4),
                    lhsT_scale=w_scales[:, g, m],
                    rhs=codes,
                    rhs_scale=scales,
                    start=(g == 0),
                    stop=(g == Z_PASSES - 1),
                )

        def O(blk, b, pair, on_v=()):
            cols, width = cols_of(blk)
            per_bank = 1 if blk == len(BLOCKS) - 1 else 512 // width
            osb = take("osb", (blk, b, pair))[:, : 2 * width].rearrange("p (k n) -> p k n", k=2)
            for k in (0, 1):
                j = 2 * pair + k
                acc = take("bank", ("S", blk, b, pair, k // per_bank * per_bank))
                src = acc[:, k % per_bank * width : (k % per_bank + 1) * width]
                if k in on_v:
                    nc.vector.tensor_scalar(out=osb[:, k, :], in0=src, scalar1=bias_sb[:, j : j + 1], scalar2=None, op0=ALU.add)
                else:
                    nc.scalar.activation(out=osb[:, k, :], in_=src, func=ACT.Identity, bias=bias_sb[:, j : j + 1])
            nc.sync.dma_start(out=out_v[b][:, 2 * pair : 2 * pair + 2, cols], in_=osb)

        nc.vector.memset(warm[:], 0.0)
        nc.scalar.activation(out=warm[:], in_=warm[:], func=ACT.Relu)
        nc.sync.dma_start(out=scale_sb[:], in_=mix_scale.rearrange("(c p t) o -> p c (t o)", p=P, t=PACK))
        LM(0, 0, 512)
        LX(0, 0)
        LX(0, 1)
        LM(1, 0, 512)
        LM(2, 0, 512)
        LX(1, 0)
        LX(1, 1)
        LW()
        LX(2, 0)
        LX(2, 1)
        LS(0, 0, 1024)
        LS(1, 0, 1024)
        LX(3, 1)
        LX(3, 0)
        LM(1, 512, 1024)
        LM(0, 512, 1024)
        LM(2, 512, 1024)
        nc.gpsimd.tensor_copy(out=bias_sb[:], in_=bias_bf[:])
        with tc.manual_schedule():
            W(0, 1, (0, 1, 2, 3,))
            W(0, 0)
            T(0, 0, 0)
            T(0, 1, 0)
            E(0, 0, 0)
            T(0, 0, 1)
            T(0, 2, 0)
            E(0, 1, 0)
            I(0, 0)
            T(0, 2, 1)
            W(0, 2, (0, 1, 2,))
            T(0, 1, 1)
            T(1, 0, 0)
            E(0, 0, 1)
            T(1, 2, 0)
            E(0, 2, 0)
            T(1, 1, 0)
            MQ(0, 0)
            Q(0, 0)
            E(0, 1, 1)
            E(1, 0, 0)
            T(1, 2, 1)
            I(0, 1)
            T(1, 0, 1)
            T(1, 1, 1)
            W(1, 0, (0, 1, 2,))
            Q(0, 1)
            MQ(0, 1)
            E(0, 2, 1, True)
            T(4, 1, 1)
            E(1, 2, 0)
            I(0, 2)
            E(1, 2, 1)
            E(1, 0, 1)
            T(4, 0, 1)
            I(1, 0, True)
            Q(0, 2)
            E(1, 1, 0)
            T(4, 0, 0)
            T(4, 1, 0)
            W(1, 2, (0, 1, 2, 3,))
            MQ(0, 2)
            M(0, 0, 1)
            Q(1, 0)
            I(1, 2, True)
            MQ(1, 0)
            E(4, 1, 1)
            E(1, 1, 1, True)
            Q(1, 1)
            E(4, 1, 0)
            W(1, 1, (0, 1, 2,))
            Q(1, 2)
            T(2, 2, 0)
            E(4, 0, 0)
            T(2, 0, 0)
            A(0, 0, 1)
            Q(4, 1)
            E(4, 0, 1)
            MQ(1, 2)
            Q(4, 0)
            E(2, 2, 0)
            M(0, 0, 0)
            M(0, 1, 1)
            T(2, 2, 1)
            E(2, 0, 0)
            T(2, 0, 1)
            M(0, 1, 0)
            A(0, 0, 0)
            A(0, 1, 1)
            R(0, 0)
            E(2, 2, 1, True)
            T(2, 1, 0)
            E(2, 0, 1)
            A(0, 1, 0)
            ZQ(0, 0)
            Q(2, 0)
            T(2, 1, 1)
            I(1, 1, True)
            T(3, 1, 1)
            T(3, 2, 1)
            MQ(1, 1)
            T(3, 0, 0)
            R(0, 1)
            Q(2, 2)
            ZQ(0, 1)
            T(3, 2, 0)
            E(2, 1, 1)
            E(2, 1, 0)
            T(3, 1, 0)
            E(3, 2, 1)
            S2(0, 0, 0)
            T(3, 0, 1)
            Q(2, 1)
            W(2, 0, (0, 1, 2,))
            S2(0, 0, 1)
            E(3, 1, 1)
            W(2, 2)
            W(3, 0)
            I(2, 2, True)
            E(3, 2, 0, True)
            E(3, 1, 0, True)
            E(3, 0, 0, True)
            E(3, 0, 1, True)
            M(0, 2, 0)
            O(0, 0, 0)
            Q(3, 1)
            M(0, 2, 1)
            I(2, 0, True)
            Q(3, 2)
            Q(3, 0)
            M(1, 1, 0)
            M(0, 3, 0)
            A(0, 2, 0)
            M(0, 3, 1)
            M(1, 0, 0)
            A(0, 2, 1)
            O(0, 0, 1)
            M(1, 1, 1)
            M(1, 2, 1)
            A(0, 3, 0)
            W(2, 1, (0,))
            A(0, 3, 1)
            M(1, 2, 0)
            A(1, 1, 0)
            R(0, 3)
            R(0, 2)
            MQ(2, 0)
            MQ(2, 2)
            ZQ(0, 3)
            M(1, 0, 1)
            M(1, 3, 1)
            M(1, 3, 0)
            W(3, 1, (0, 1,))
            A(1, 2, 1)
            A(1, 1, 1)
            I(2, 1, True)
            A(1, 0, 1)
            I(3, 0, True)
            MQ(2, 1)
            A(1, 0, 0)
            R(1, 1)
            W(3, 2)
            M(2, 0, 1)
            A(1, 2, 0)
            ZQ(1, 1)
            ZQ(0, 2)
            R(1, 0)
            R(1, 2)
            MQ(3, 0)
            A(1, 3, 1)
            M(2, 1, 0)
            ZQ(1, 0)
            M(2, 0, 0)
            A(2, 0, 1)
            I(3, 1, True)
            I(3, 2, True)
            S2(0, 1, 1)
            M(2, 2, 1)
            A(1, 3, 0)
            MQ(3, 1)
            M(2, 1, 1)
            O(0, 1, 1)
            S2(0, 1, 0)
            A(2, 0, 0)
            A(2, 1, 0)
            MQ(3, 2)
            ZQ(1, 2)
            R(1, 3)
            M(2, 2, 0)
            M(2, 3, 0)
            M(2, 3, 1)
            M(3, 0, 0)
            R(2, 0)
            A(2, 2, 1)
            S2(1, 0, 0)
            M(3, 1, 1)
            A(2, 2, 0)
            A(2, 1, 1)
            O(0, 1, 0)
            M(3, 1, 0)
            ZQ(1, 3)
            R(2, 1)
            A(2, 3, 1)
            O(1, 0, 0)
            S2(1, 0, 1)
            ZQ(2, 1)
            R(2, 2)
            M(3, 0, 1)
            A(2, 3, 0)
            S2(1, 1, 1)
            O(1, 0, 1)
            S2(1, 1, 0)
            A(3, 0, 0)
            O(1, 1, 0)
            A(3, 1, 1)
            ZQ(2, 2)
            ZQ(2, 0)
            M(3, 3, 1)
            R(2, 3)
            M(3, 2, 0)
            A(3, 0, 1)
            A(3, 1, 0)
            O(1, 1, 1)
            ZQ(2, 3)
            M(3, 3, 0)
            A(3, 3, 1)
            A(3, 3, 0)
            S2(2, 1, 1)
            R(3, 0)
            R(3, 1)
            S2(2, 0, 1)
            ZQ(3, 0)
            A(3, 2, 0)
            O(2, 1, 1)
            R(3, 3)
            S2(2, 0, 0)
            M(3, 2, 1)
            O(2, 0, 0)
            S2(2, 1, 0)
            A(3, 2, 1)
            ZQ(3, 1)
            S2(3, 0, 0)
            ZQ(3, 3)
            O(2, 0, 1)
            O(2, 1, 0)
            R(3, 2)
            S2(3, 0, 1)
            O(3, 0, 0, (0,))
            ZQ(3, 2)
            S2(3, 1, 1)
            O(3, 0, 1, (0,))
            S2(3, 1, 0)
            O(3, 1, 1, (0,))
            O(3, 1, 0, (0,))
